import numpy as np, ml_dtypes
CORES = [10,34,74,98]
N = 4
BF = ml_dtypes.bfloat16
B, S, D, SH = 4, 4096, 8192, 4
W, BC = N * B, 16
LAST = (2 * 255 * 255) >> SH
def middle(m):
    return 16 * (m % 16) + 8, 16 * (m // 16) + 8
def index(p, x, y):
    return ((x - int(p[0])) ** 2 + (y - int(p[1])) ** 2) >> SH
def loud(d, rng, cells):
    t = rng.integers(0, S, (N, 8)); sg = rng.choice(np.array([-15.0, 15.0]), 16); v = d["tr"].reshape(N, 8, 16, S); x, y = middle(np.array(cells))
    ld = sg - np.sign(sg) * rng.integers(0, 2, (N, 8, 16))
    for q in range(N):
        for g in range(8):
            d["tau"][q, g, index(d["pos"][q, g], x, y)] = t[q, g]; v[q, g, :, t[q, g]] = ld[q, g].astype(BF)
    return t, ld
def setup_inputs(rng):
    tr = rng.integers(-15, 16, (N, 128, S), dtype=np.int8).astype(np.float32).astype(BF)
    pos = rng.integers(0, 256, (N, 8, 2)).astype(np.int32)
    t = np.floor(np.sqrt(np.arange(D) / D) * (rng.random((N, 8, 1)) * 0.5 + 0.25) * S).astype(np.int64) + rng.integers(0, S // 4, (N, 8, D))
    return {"tr": tr, "pos": pos, "tau": t.astype(np.int32)}
def setup_inputs_ends(rng):
    d = setup_inputs(rng); c = np.array([[0, 0], [0, 255], [255, 0], [255, 255]])
    d["pos"] = np.stack([c[rng.permutation(8) % 4] for q in range(N)]).astype(np.int32)
    t = rng.integers(0, S, (N, 8, D)); t[:, :, 0] = 0; t[:, :, LAST] = S - 1; d["tau"] = t.astype(np.int32)
    e = rng.integers(0, 2, W); e[0] = 0; e[W - 1] = 1
    loud(d, rng, np.arange(W) * BC + e * (BC - 1)); return d
def setup_inputs_ties(rng):
    d = setup_inputs(rng); s = int(rng.integers(0, 3)); cells = []
    for k in range(W):
        z = (k + s) % 3; o = [0, BC - 1] if z == 0 else rng.choice(BC, 2, replace=False) if z == 1 else range(BC)
        cells += [k * BC + int(i) for i in o]
    loud(d, rng, cells); return d
def setup_inputs_close(rng):
    d = setup_inputs(rng); k = np.arange(W); lo = k * BC + rng.integers(0, BC // 2, W); hi = k * BC + BC // 2 + rng.integers(0, BC // 2, W); x, y = middle(lo)
    d["pos"][k % N, k // N, 0] = x; d["pos"][k % N, k // N, 1] = y
    t, ld = loud(d, rng, np.concatenate([lo, hi])); v = d["tr"].reshape(N, 8, 16, S); m = np.abs(np.sum(ld, axis=(0, 1)))
    for i in range(W):
        q, g = i % N, i // N; u = (int(t[q, g]) + int(rng.integers(1, S))) % S; h = ld[q, g].copy(); s = int(rng.integers(0, 16))
        if i % 2:
            z = [(m[a] - m[b], a, b) for a in range(16) for b in range(16) if m[a] > m[b] + 1 and abs(h[b]) < 15]
            if z:
                s, b = min(z)[1:]; h[b] = h[b] + np.sign(h[b])
        h[s] = h[s] - np.sign(h[s])
        d["tau"][q, g, 0] = u; v[q, g, :, u] = h.astype(BF)
    return d
def setup_inputs_steps(rng):
    d = setup_inputs(rng); d["pos"] = np.repeat(rng.integers(0, 256, (N, 1, 2)), 8, axis=1).astype(np.int32)
    d["tau"] = np.repeat(rng.integers(0, S, (N, 8, D // 64)), 64, axis=2).astype(np.int32); return d
def setup_inputs_spread(rng):
    d = setup_inputs(rng); a = rng.choice(np.array([0, 1, 4, 15], np.int8), (N, 8, 1, S))
    v = np.clip(rng.integers(-15, 16, (N, 8, 16, S), dtype=np.int8), -a, a)
    d["tr"] = v.reshape(N, 128, S).astype(np.float32).astype(BF)
    d["pos"] = np.floor(256 * rng.random((N, 8, 2)) ** 3).astype(np.int32); d["tau"] = np.floor(S * rng.random((N, 8, D)) ** 3).astype(np.int32); return d
def check_inputs(d):
    bad = []; v = np.asarray(d["tr"]).astype(np.float32)
    if not ((np.abs(v) <= 15) & (np.rint(v) == v)).all(): bad.append("samples")
    if not ((d["pos"] >= 0) & (d["pos"] <= 255)).all(): bad.append("places")
    if not ((d["tau"] >= 0) & (d["tau"] < S)).all(): bad.append("times")
    return bad
def focus(v, pos, tau, x, y):
    a = np.zeros((16, len(x)), np.int64)
    for q in range(N):
        for g in range(8): a += v[q, g][:, tau[q, g][index(pos[q, g], x, y)]]
    return a
def reference(tr, pos, tau):
    v = tr.astype(np.float32).astype(np.int32).reshape(N, 8, 16, S)
    x, y = middle(np.arange(256)); c = focus(v, pos, tau, x, y)
    e = np.sum(c * c, axis=0).reshape(W, BC)
    w = np.arange(W) * BC + np.argmax(e, axis=1)
    j = np.arange(256); x = (16 * (w % 16)[:, None] + j % 16).reshape(-1); y = (16 * (w // 16)[:, None] + j // 16).reshape(-1)
    fine = focus(v, pos, tau, x, y).reshape(16, N, B * 256).transpose(1, 0, 2)
    return {"y": np.ascontiguousarray(fine).astype(np.float32), "w": np.tile(w.reshape(1, 1, W), (N, 1, 1)).astype(np.float32)}

@@ -1,0 +1,284 @@
+import numpy as np
+from concourse.bass import DstId, RemoteDMATransfer
+from concourse.mybir import AluOpType as A, AxisListType, ActivationFunctionType as AF
+
+N = 4
+MAGIC = 12582912.0
+TOT = 509
+T2V0, T2V1, T2M, T2V2 = 8, 16, 4, 13
+T2V = (178,)
+T2S = (102, 102)
+OLB = 13
+PARTS = [[4], [3, 1], [2, 1], [1, 3]]
+PARTS_S = [[4], [4], [3, 2], [2, 2]]
+SCRATCH = {
+    "TR": ("sbuf", [128, 4096], "bfloat16"), "T2": ("sbuf", [128, 8192], "bfloat16"),
+    "TIA": ("sbuf", [128, 16, 16], "int32"), "TIB": ("sbuf", [128, 16, 16], "int32"),
+    "X": ("sbuf", [128, 16, 32], "float32"), "XT": ("sbuf", [128, 512], "float32"), "OL": ("sbuf", [128, 512], "uint16"),
+    "POSI": ("sbuf", [128, 2], "int32"), "POSB": ("sbuf", [128, 2], "bfloat16"),
+    "pI": ("sbuf", [128, 1], "int32"), "rI": ("sbuf", [128, 1], "int32"), "eI": ("sbuf", [128, 1], "int32"),
+    "dI": ("sbuf", [128, 1], "int32"), "pF": ("sbuf", [128, 1], "float32"), "rF": ("sbuf", [128, 1], "float32"),
+    "eF": ("sbuf", [128, 1], "float32"), "dF": ("sbuf", [128, 1], "float32"), "b16": ("sbuf", [128, 1], "float32"),
+    "k16": ("sbuf", [128, 1], "float32"), "r8": ("sbuf", [128, 1], "float32"),
+    "CF": ("sbuf", [128, 256], "bfloat16"), "C16": ("sbuf", [128, 256], "bfloat16"), "J16": ("sbuf", [128, 128], "bfloat16"),
+    "IDF": ("sbuf", [128, 128], "float32"), "IDB": ("sbuf", [128, 128], "bfloat16"), "SEL": ("sbuf", [128, 16], "bfloat16"),
+    "ONE": ("sbuf", [128, 16], "bfloat16"), "BCT": ("sbuf", [128, 128], "bfloat16"), "M8": ("sbuf", [128, 8], "float32"),
+    "NK": ("sbuf", [128, 16], "float32"), "REP": ("sbuf", [128, 256], "float16"), "LM": ("sbuf", [128, 144], "float16"),
+    "SB": ("sbuf", [128, 136], "bfloat16"),
+    "XY8": ("sbuf", [128, 2], "float32"), "XYQ": ("sbuf", [128, 2], "float32"), "XB": ("sbuf", [128, 1], "float32"),
+    "XR": ("sbuf", [128, 1], "float32"),
+    "XQ": ("sbuf", [128, 1], "float32"), "XM": ("sbuf", [128, 1], "float32"), "DX": ("sbuf", [128, 128], "bfloat16"),
+    "SXC": ("sbuf", [128, 16], "float32"), "SQX": ("sbuf", [128, 128], "float32"), "SYC": ("sbuf", [128, 1], "float32"),
+    "SQF": ("sbuf", [128, 256], "float32"),
+    "SR": ("sbuf", [128, 128], "int32"), "LOW": ("sbuf", [128, 128], "int32"), "MK": ("sbuf", [128, 128], "float32"),
+    "SCI": ("sbuf", [128, 16], "int32"), "SCH": ("sbuf", [128, 16], "int32"), "SCL": ("sbuf", [128, 16], "int32"),
+    "SCP": ("sbuf", [128, 16], "int32"), "LN": ("sbuf", [128, 16], "uint16"),
+    "GM": ("sbuf", [128, 256], "float16"), "CL": ("sbuf", [128, 16], "uint16"), "CG": ("sbuf", [128, 256], "bfloat16"),
+    "CS": ("sbuf", [128, 32], "bfloat16"),
+    "I0A": ("sbuf", [128, 256], "float32"), "I0B": ("sbuf", [128, 256], "float32"), "I0F": ("sbuf", [128, 256], "float32"),
+    "JUNK": ("sbuf", [128, 32], "float32"), "EN": ("sbuf", [128, 2], "float32"), "RE": ("sbuf", [128, 16], "float32"),
+    "MN": ("sbuf", [128, 1], "float32"), "U": ("sbuf", [128, 16], "float32"), "SC": ("sbuf", [128, 16], "float32"),
+    "WT": ("sbuf", [128, 1], "float32"), "WK": ("sbuf", [128, 128], "float16"),
+    "IDX": ("sbuf", [128, 256], "uint16"), "F": ("sbuf", [128, 4096], "bfloat16"), "FS": ("sbuf", [128, 384], "bfloat16"),
+    "YS": ("sbuf", [128, 128], "float32"),
+    "PA": ("psum", [128, 512], "float32"), "PB": ("psum", [128, 512], "float32"), "PC": ("psum", [128, 512], "float32"),
+    "PY": ("psum", [128, 512], "float32"),
+}
+for _q in range(N):
+    SCRATCH["Q%d" % _q] = ("psum", [128, 512], "float32")
+    SCRATCH["CR%d" % _q] = ("sbuf", [128, 32], "bfloat16")
+    SCRATCH["FR%d" % _q] = ("sbuf", [128, 128], "bfloat16")
+SEMAPHORES = ["v", "s", "p", "c", "dpos", "dta", "dtb", "dtr", "dw", "dy", "lc", "lf"]
+SEMAPHORES += ["ca%d" % _q for _q in range(N)] + ["fa%d" % _q for _q in range(N)]
+
+
+def rank_program(g, core, T, topo):
+    rank = T.rank_of(core)
+    if rank is None:
+        return
+    cores = T.cores
+    chip = topo.chip(core)
+    queue = {"v": g.vector, "s": g.scalar, "p": g.tensor, "c": g, "y": g.sync}
+    count = {"v": 0, "s": 0, "p": 0, "c": 0}
+    seen = {}
+
+    def wait(q, *deps):
+        for name, val in deps:
+            if seen.get((q, name), 0) < val:
+                seen[(q, name)] = val
+                queue[q].wait_ge(T.sem[name], val)
+
+    def op(q, deps, make):
+        wait(q, *deps)
+        make(queue[q]).then_inc(T.sem[q], 1)
+        count[q] += 1
+        return (q, count[q])
+
+    def V(deps, make): return op("v", deps, make)
+    def ts(deps, out, in0, s1, s2, o0, o1=None):
+        if o1 is None:
+            return V(deps, lambda e: e.tensor_scalar(out, in0, s1, None, o0))
+        return V(deps, lambda e: e.tensor_scalar(out, in0, s1, s2, o0, o1))
+    def tt(deps, out, a, b, o): return V(deps, lambda e: e.tensor_tensor(out, a, b, o))
+    def cp(deps, out, in_): return V(deps, lambda e: e.tensor_copy(out, in_))
+    def act(deps, out, in_, func, **kw): return op("s", deps, lambda e: e.activation(out, in_, func, **kw))
+    def mm(deps, out, lhsT, rhs, start, stop): return op("p", deps, lambda e: e.matmul(out, lhsT, rhs, start, stop))
+
+    others = sorted([q for q in range(N) if q != rank],
+                    key=lambda q: (topo.same_plane(chip, topo.chip(cores[q])), q ^ rank))
+    order = others + [rank]
+
+    g.sync.dma_start(T.POSI[0:8, :], T.pos[:]).then_inc(T.sem.dpos, 16)
+    g.scalar.dma_start(T.TIA[:], T.tau[0:8:2, :]).then_inc(T.sem.dta, 16)
+    g.sync.dma_start(T.TIB[:], T.tau[1:8:2, :]).then_inc(T.sem.dtb, 16)
+    g.sync.dma_start(T.TR[:], T.tr[:]).then_inc(T.sem.dtr, 16)
+    pos_in, ta_in, tb_in, tr_in = ("dpos", 16), ("dta", 16), ("dtb", 16), ("dtr", 16)
+
+    def iota(out, pattern, cm, flag):
+        if flag:
+            return op("c", [], lambda e: e.iota(out, pattern, 0, cm, allow_small_or_imprecise_dtypes=True))
+        return op("c", [], lambda e: e.iota(out, pattern, 0, cm))
+    k_p = iota(T.pI[:], [[0, 1]], 1, False)
+    k_c16 = iota(T.C16[:, 0:128], [[1, 8], [0, 16]], 0, True)
+    k_cf = iota(T.CF[:, 0:144], [[1, 144]], 0, True)
+    k_j16 = iota(T.J16[:], [[0, 8], [1, 16]], 0, True)
+    a_one = V([], lambda e: e.memset(T.ONE[:], 1.0))
+    a_pf = cp([k_p], T.pF[:], T.pI[:])
+    a_ri = ts([k_p], T.rI[:], T.pI[:], 15, None, A.bitwise_and)
+    a_ei = ts([k_p], T.eI[:], T.pI[:], 7, None, A.bitwise_and)
+    a_di = ts([k_p], T.dI[:], T.pI[:], 3, None, A.logical_shift_right)
+    a_rf = cp([a_ri], T.rF[:], T.rI[:])
+    a_bc = ts([k_c16, a_pf], T.BCT[0:8, :], T.C16[0:8, 0:128], T.pF[0:8, :], None, A.is_equal)
+    a_b16 = tt([a_pf, a_rf], T.b16[:], T.pF[:], T.rF[:], A.subtract)
+    a_ef = cp([a_ei], T.eF[:], T.eI[:])
+    a_df = cp([a_di], T.dF[:], T.dI[:])
+    a_c16 = act([k_c16], T.C16[0:16, 128:256], T.C16[0:16, 0:128], AF.Identity, bias=8.0)
+    a_k16 = act([a_pf], T.k16[:], T.pF[:], AF.Identity, scale=16.0)
+    a_r8 = act([a_rf], T.r8[:], T.rF[:], AF.Identity, scale=8.0)
+    a_cf = act([k_cf], T.CF[:, 144:256], T.CF[:, 32:144], AF.Identity, bias=112.0)
+    ts([], T.REP[0:16, 0:128], T.C16[0:16, 0:128], T.pF[0:16, :], 16.0, A.is_equal, A.mult)
+    a_rep = ts([a_c16], T.REP[0:16, 128:256], T.C16[0:16, 128:256], T.pF[0:16, :], 16.0, A.is_equal, A.mult)
+    a_lm = ts([k_cf, a_b16], T.LM[:], T.CF[:, 0:144], T.b16[:], 15.0, A.subtract, A.is_equal)
+    b_pos = ts([pos_in], T.POSB[0:8, :], T.POSI[0:8, :], -1.0, None, A.mult)
+    b_nxy = mm([b_pos, a_bc], T.PA[:, 0:2], T.BCT[0:8, :], T.POSB[0:8, :], True, True)
+    s_xy8 = act([b_nxy], T.XY8[:], T.PA[:, 0:2], AF.Identity, bias=8.0)
+    cx, cy = T.XY8[:, 0:1], T.XY8[:, 1:2]
+    s_sxc = act([s_xy8, k_cf], T.SXC[:], T.CF[:, 0:16], AF.Square, bias=cx, scale=16.0)
+    s_syc = act([a_rf], T.SYC[:], T.rF[:], AF.Square, bias=cy, scale=16.0)
+    s_sqx = act([k_c16], T.SQX[:], T.C16[:, 0:128], AF.Square, bias=cx, scale=16.0)
+    s_sqy = act([k_j16], T.PB[:, 0:128], T.J16[:], AF.Square, bias=cy, scale=16.0)
+    t_a = ts([ta_in], T.X[:, :, 0:16], T.TIA[:], -2048.0, None, A.add)
+    a_m8 = ts([a_ef, k_cf], T.M8[:], T.CF[:, 0:8], T.eF[:], 7.0, A.add, A.is_equal)
+    t_b = ts([tb_in], T.X[:, :, 16:32], T.TIB[:], -2048.0, None, A.add)
+    s_xyq = act([s_xy8], T.XYQ[:], T.XY8[:], AF.Identity, bias=-2.0, scale=0.25)
+    s_xq = act([s_xyq, a_rf], T.XQ[:], T.rF[:], AF.Square, bias=T.XYQ[:, 0:1], scale=0.25)
+    s_sqf = act([a_cf], T.SQF[:], T.CF[:], AF.Square, bias=T.XYQ[:, 1:2], scale=0.25)
+    s_xm = act([s_xq], T.XM[:], T.XQ[:], AF.Identity, bias=-0.46875)
+    s_xb = act([], T.XB[:], T.XYQ[:, 0:1], AF.Identity, scale=0.5)
+    s_ia = act([s_xm, s_sqf], T.I0A[:], T.SQF[:], AF.Identity, bias=T.XM[:])
+    b_xr = act([s_xb], T.XR[:], T.rF[:], AF.Identity, bias=T.XB[:], scale=0.125)
+    s_ib = act([s_ia], T.I0B[:], T.I0A[:], AF.Identity, bias=MAGIC)
+    s_i0 = act([s_ib], T.I0F[:], T.I0B[:], AF.Identity, bias=-MAGIC)
+    b_sc = ts([s_sxc, s_syc], T.SCI[:], T.SXC[:], T.SYC[:], None, A.add)
+    a_nk = ts([a_df], T.NK[:], T.CF[:, 0:16], T.dF[:], -1.0, A.is_equal, A.mult)
+    a_sb = ts([a_r8], T.SB[:], T.CF[:, 0:136], T.r8[:], 7.0, A.subtract, A.is_equal)
+    b_sr = tt([s_sqx, s_sqy], T.SR[:], T.PB[:, 0:128], T.SQX[:], A.add)
+    t_x = V([t_a, t_b], lambda e: e.transpose(T.XT[:], T.X[:]))
+    b_sh = ts([b_sc], T.SCH[:], T.SCI[:], 3, 480, A.logical_shift_right, A.bitwise_and)
+    b_sl = ts([b_sc], T.SCL[:], T.SCI[:], 12, None, A.logical_shift_right)
+    b_low = ts([b_sr], T.LOW[:], T.SR[:], 4, 15, A.logical_shift_right, A.bitwise_and)
+    b_sp = tt([b_sh, b_sl], T.SCP[:], T.SCH[:], T.SCL[:], A.add)
+    a_idb = ts([k_cf, a_pf], T.IDB[:], T.CF[:, 0:128], T.pF[:], None, A.is_equal)
+    b_mk = ts([b_low, a_rf], T.MK[:], T.LOW[:], T.rF[:], None, A.is_equal)
+    b_ln = cp([b_sp], T.LN[:], T.SCP[:])
+    a_sel = ts([k_cf, a_rf], T.SEL[:], T.CF[:, 0:16], T.rF[:], None, A.is_equal)
+    a_idf = act([a_idb], T.IDF[:], T.IDB[:], AF.Identity)
+    b_dx = act([b_xr], T.DX[:], T.IDB[:], AF.Identity, scale=T.XR[:])
+    c_gm = [tt([t_x, b_ln, b_mk], T.GM[:, h:h + 128], T.XT[:, 0:512].indirect(T.LN[:, h // 16:h // 16 + 8]), T.MK[:], A.mult)
+            for h in (0, 128)]
+    c_re = None
+    for r in range(16):
+        c_re = mm([c_gm[r // 8], a_lm], T.PC[:, 0:16], T.LM[:, 15 - r:143 - r], T.GM[:, 16 * r:16 * r + 16], r == 0, r == 15)
+    def times(b): return ts([t_x], T.OL[:, b:512:16], T.XT[:, 32 * b:32 * b + 32], 2048.0, None, A.add)
+    t_ol = None
+    for b in range(OLB):
+        times(b)
+    c_cl = ts([c_re], T.CL[:], T.PC[:, 0:16], 2048.0, None, A.add)
+    for b in range(OLB, 16):
+        t_ol = times(b)
+    col, last = [0], {}
+
+    def piece(q, n):
+        a, e = col[0], col[0] + n
+        col[0] = e
+        out, in_ = T.T2[:, 16 * a:16 * e], T.TR[:, 0:4096].indirect(T.OL[:, a:e])
+        last[q] = cp([t_ol, tr_in], out, in_) if q == "v" else act([t_ol, tr_in], out, in_, AF.Copy)
+    c_gv = cp([tr_in, c_cl], T.CG[:, 0:128], T.TR[:, 0:4096].indirect(T.CL[:, 0:8]))
+    c_gs = act([tr_in, c_cl], T.CG[:, 128:256], T.TR[:, 0:4096].indirect(T.CL[:, 8:16]), AF.Copy)
+    mm([c_gv, c_gs, a_sel], T.PC[:, 32:48], T.CG[:, 0:256:2], T.SEL[:], True, True)
+    c_ps = mm([], T.PC[:, 48:64], T.CG[:, 1:256:2], T.SEL[:], True, True)
+    piece("v", T2V0)
+    c_cs = cp([c_ps], T.CS[:], T.PC[:, 32:64])
+    mask = 0xFFFF
+    for q in others:
+        mask &= topo.mask(core, cores[q])
+    n_e = bin(mask).count("1")
+
+    def dst(q):
+        rid, pid, _ = topo.addr(cores[q])
+        return DstId(rid=rid, pnc=pid)
+    wait("c", c_cs)
+    g.remote_dma_fused([RemoteDMATransfer(dst_ids=[dst(q) for q in others], dma_engine_mask=mask, remote_sem=T.sem["ca%d" % rank],
+                                          srcs=[T.CS[:]], dsts=[T["CR%d" % rank][:] for q in others], alu_op=0)],
+                       local_sem=T.sem.lc)
+    for n in T2V:
+        piece("v", n)
+    for n in T2S:
+        piece("s", n)
+    b_xp = mm([b_dx, a_one], T.PA[0:16, 128:256], T.ONE[:], T.DX[:], True, True)
+    e_a = mm([c_cs, a_idb], T.PB[:, 256:288], T.IDB[:], T.CS[:], True, False)
+    for t, q in enumerate(order):
+        mm([s_i0, a_idf], T["Q%d" % t][:, 0:64], T.IDF[:], T.I0F[:, 64 * q:64 * q + 64], True, False)
+    for n, q in enumerate(others):
+        e_a = mm([("ca%d" % q, n_e)], T.PB[:, 256:288], T.IDB[:], T["CR%d" % q][:], False, n == N - 2)
+    e_0 = act([e_a], T.JUNK[:, 0:16], T.PB[:, 256:272], AF.Square, accum_out=T.EN[:, 0:1])
+    e_1 = act([], T.JUNK[:, 16:32], T.PB[:, 272:288], AF.Square, accum_out=T.EN[:, 1:2])
+    piece("s", TOT - col[0] - T2V1 - 3 * T2M - T2V2)
+    ts([e_0, a_m8], T.RE[:, 1:16:2], T.M8[:], T.EN[:, 0:1], None, A.mult)
+    e_r = ts([e_1], T.RE[:, 0:16:2], T.M8[:], T.EN[:, 1:2], None, A.mult)
+    e_e = mm([e_r, a_nk], T.PB[0:16, 320:336], T.NK[:], T.RE[:], True, True)
+    piece("v", T2V1)
+    w_m = V([e_e], lambda e: e.tensor_reduce(T.MN[0:16, :], T.PB[0:16, 320:336], AxisListType.X, A.min))
+    piece("v", T2M)
+    w_u = ts([w_m], T.U[0:16, :], T.PB[0:16, 320:336], T.MN[0:16, :], 1.0, A.subtract, A.min)
+    piece("v", T2M)
+    w_s = V([w_u], lambda e: e.tensor_tensor_scan(T.SC[0:16, :], T.U[0:16, :], T.U[0:16, :], 0.0, A.mult, A.add))
+    piece("v", T2M)
+    acol = T.SC[0:16, 15:16]
+    w_k = ts([w_s, b_xp], T.WK[0:16, :], T.PA[0:16, 128:256], acol, acol, A.add, A.mult)
+    piece("v", T2V2)
+    i_q = []
+    for t, q in enumerate(order):
+        i_q.append(mm([w_k, a_rep], T["Q%d" % t][:, 0:64], T.WK[0:16, :], T.REP[0:16, 64 * q:64 * q + 64], False, True))
+    idx, got, fp, fs = [], [{} for _ in range(N)], [None] * N, [None] * N
+
+    def index(t):
+        q = order[t]
+        idx.append(cp([i_q[t]], T.IDX[:, 64 * q:64 * q + 64], T["Q%d" % t][:, 0:64]))
+
+    def gather(t, kind, part):
+        q, parts = order[t], PARTS[t] if kind == "v" else PARTS_S[t]
+        b = sum(parts[:part]) + (0 if kind == "v" else sum(PARTS[t]))
+        lo, hi = 64 * q + 8 * b, 64 * q + 8 * (b + parts[part])
+        deps, out, in_ = [idx[t], last["v"], last["s"]], T.F[:, 16 * lo:16 * hi], T.T2[:, 0:16 * TOT].indirect(T.IDX[:, lo:hi])
+        c = cp(deps, out, in_) if kind == "v" else act(deps, out, in_, AF.Copy)
+        for i in range(b, b + parts[part]):
+            got[t][i] = c
+
+    def gathers(t, kind):
+        for part in range(len(PARTS[t] if kind == "v" else PARTS_S[t])):
+            gather(t, kind, part)
+
+    def blocks(t):
+        base = {k: min(c[1] for c in got[t].values() if c[0] == k) for k in "vs"}
+        return sorted(range(8), key=lambda b: (got[t][b][1] != base[got[t][b][0]], got[t][b][0], b))
+
+    def sums(t):
+        q = order[t]
+        for b in blocks(t):
+            fp[t] = mm([got[t][b], a_sel], T["Q%d" % t][:, 128 + b:256:8],
+                       T.F[:, 1024 * q + 128 * b:1024 * q + 128 * b + 128], T.SEL[:], True, True)
+
+    def out(t):
+        q = order[t]
+        fs[t] = cp([fp[t]], T.FS[:, 128 * t:128 * t + 128], T["Q%d" % t][:, 128:256])
+        wait("c", fs[t])
+        rid, pid, _ = topo.addr(cores[q])
+        g.remote_dma(T["FR%d" % rank][:], T.FS[:, 128 * t:128 * t + 128], T.sem["fa%d" % rank], T.sem.lf, pid, rid,
+                     topo.mask(core, cores[q]))
+    index(0); index(1); index(2); index(3)
+    gathers(0, "v"); gathers(0, "s")
+    sums(0)
+    for t in (1, 2, 3):
+        gather(t, "v", 0)
+        out(t - 1)
+        gather(t, "v", 1)
+        gathers(t, "s")
+        if t < 3:
+            sums(t)
+    w_t = ts([a_k16], T.WT[0:16, :], acol, T.k16[0:16, :], None, A.add)
+    wait("y", w_t)
+    g.sync.dma_start(T.w[:], T.WT[0:16, :]).then_inc(T.sem.dw, 16)
+    for n, b in enumerate(blocks(3)):
+        mm([got[3][b], a_sb], T.PY[:, 0:128], T.SB[:, 7 - b:135 - b],
+           T.F[:, 1024 * rank + 128 * b:1024 * rank + 128 * b + 128], n == 0, False)
+    y_p = None
+    for n, q in enumerate(others):
+        y_p = mm([("fa%d" % q, bin(topo.mask(cores[q], core)).count("1"))], T.PY[:, 0:128], T["FR%d" % q][:], T.IDB[:], False, n == N - 2)
+    y_s = cp([y_p], T.YS[:], T.PY[:, 0:128])
+    wait("y", y_s)
+    g.sync.dma_start(T.y[:], T.YS[:]).then_inc(T.sem.dy, 16)
+    wait("y", ("dw", 16), ("dy", 16))
+    lf = sum(bin(topo.mask(core, cores[q])).count("1") for q in others)
+    wait("c", ("lc", n_e), ("lf", lf))
+    wait("c", ("v", count["v"]), ("s", count["s"]), ("p", count["p"]), ("c", count["c"]))

@@ -1,53 +1,47 @@
-import numpy as np
 from concourse.bass import DstId, RemoteDMATransfer
-from concourse.mybir import AluOpType as A, AxisListType, ActivationFunctionType as AF
+from concourse.mybir import AluOpType as A, ActivationFunctionType as AF
 
 N = 4
-MAGIC = 12582912.0
 TOT = 509
-T2V0, T2V1, T2M, T2V2 = 8, 16, 4, 13
-T2V = (178,)
-T2S = (102, 102)
-OLB = 13
-PARTS = [[4], [3, 1], [2, 1], [1, 3]]
-PARTS_S = [[4], [4], [3, 2], [2, 2]]
+T2A, T2B = 16, 24
+T2V, T2V1, T2V2 = 196, 10, 12
+T2S, T2S1 = 196, 22
+WA, WF, TX = 256, 0, 256
+FINE = [("s", 0, 4), ("v", 0, 4), ("s", 1, 4), ("v", 1, 4), ("v", 0, 0), ("s", 2, 1), ("v", 2, 3), ("s", 2, 3),
+        ("v", 2, 1), ("s", 1, 0), ("s", 3, 3), ("v", 2, 0), ("s", 3, 2), ("v", 3, 3)]
+ARR = (3, 8, 8)
 SCRATCH = {
     "TR": ("sbuf", [128, 4096], "bfloat16"), "T2": ("sbuf", [128, 8192], "bfloat16"),
-    "TIA": ("sbuf", [128, 16, 16], "int32"), "TIB": ("sbuf", [128, 16, 16], "int32"),
-    "X": ("sbuf", [128, 16, 32], "float32"), "XT": ("sbuf", [128, 512], "float32"), "OL": ("sbuf", [128, 512], "uint16"),
-    "POSI": ("sbuf", [128, 2], "int32"), "POSB": ("sbuf", [128, 2], "bfloat16"),
-    "pI": ("sbuf", [128, 1], "int32"), "rI": ("sbuf", [128, 1], "int32"), "eI": ("sbuf", [128, 1], "int32"),
-    "dI": ("sbuf", [128, 1], "int32"), "pF": ("sbuf", [128, 1], "float32"), "rF": ("sbuf", [128, 1], "float32"),
-    "eF": ("sbuf", [128, 1], "float32"), "dF": ("sbuf", [128, 1], "float32"), "b16": ("sbuf", [128, 1], "float32"),
-    "k16": ("sbuf", [128, 1], "float32"), "r8": ("sbuf", [128, 1], "float32"),
-    "CF": ("sbuf", [128, 256], "bfloat16"), "C16": ("sbuf", [128, 256], "bfloat16"), "J16": ("sbuf", [128, 128], "bfloat16"),
-    "IDF": ("sbuf", [128, 128], "float32"), "IDB": ("sbuf", [128, 128], "bfloat16"), "SEL": ("sbuf", [128, 16], "bfloat16"),
-    "ONE": ("sbuf", [128, 16], "bfloat16"), "BCT": ("sbuf", [128, 128], "bfloat16"), "M8": ("sbuf", [128, 8], "float32"),
-    "NK": ("sbuf", [128, 16], "float32"), "REP": ("sbuf", [128, 256], "float16"), "LM": ("sbuf", [128, 144], "float16"),
-    "SB": ("sbuf", [128, 136], "bfloat16"),
-    "XY8": ("sbuf", [128, 2], "float32"), "XYQ": ("sbuf", [128, 2], "float32"), "XB": ("sbuf", [128, 1], "float32"),
-    "XR": ("sbuf", [128, 1], "float32"),
-    "XQ": ("sbuf", [128, 1], "float32"), "XM": ("sbuf", [128, 1], "float32"), "DX": ("sbuf", [128, 128], "bfloat16"),
-    "SXC": ("sbuf", [128, 16], "float32"), "SQX": ("sbuf", [128, 128], "float32"), "SYC": ("sbuf", [128, 1], "float32"),
-    "SQF": ("sbuf", [128, 256], "float32"),
-    "SR": ("sbuf", [128, 128], "int32"), "LOW": ("sbuf", [128, 128], "int32"), "MK": ("sbuf", [128, 128], "float32"),
+    "TIA": ("sbuf", [128, 16, 16], "int32"), "TIB": ("sbuf", [128, 16, 16], "int32"), "X": ("sbuf", [128, 16, 32], "float32"),
+    "XT": ("sbuf", [128, 512], "float32"), "W": ("sbuf", [128, 512], "float32"), "OL": ("sbuf", [128, 512], "uint16"),
+    "POSI": ("sbuf", [128, 2], "int32"), "POSB": ("sbuf", [128, 2], "bfloat16"), "PL": ("sbuf", [128, 32], "uint16"),
+    "pI": ("sbuf", [128, 1], "int32"), "rI": ("sbuf", [128, 1], "int32"), "rF": ("sbuf", [128, 1], "float32"),
+    "b16": ("sbuf", [128, 1], "float32"), "k16": ("sbuf", [128, 1], "float32"), "r8": ("sbuf", [128, 1], "float32"),
+    "r32": ("sbuf", [128, 1], "float32"), "CT": ("sbuf", [128, 256], "bfloat16"), "J16": ("sbuf", [128, 128], "bfloat16"),
+    "CF": ("sbuf", [128, 144], "bfloat16"), "ONE": ("sbuf", [128, 144], "bfloat16"), "C16": ("sbuf", [128, 64], "bfloat16"),
+    "IDF": ("sbuf", [128, 128], "float32"), "IDB": ("sbuf", [128, 128], "bfloat16"), "SELP": ("sbuf", [128, 48], "bfloat16"),
+    "BCT": ("sbuf", [128, 128], "bfloat16"), "S8": ("sbuf", [128, 8], "float32"),
+    "REP": ("sbuf", [128, 256], "bfloat16"), "LM": ("sbuf", [128, 144], "float16"), "SB": ("sbuf", [128, 136], "bfloat16"),
+    "XY8": ("sbuf", [128, 2], "float32"), "XYQ": ("sbuf", [128, 2], "float32"), "XL": ("sbuf", [128, 16], "bfloat16"),
+    "XQ": ("sbuf", [128, 1], "float32"), "XM": ("sbuf", [128, 1], "float32"), "XP": ("sbuf", [128, 128], "bfloat16"),
+    "SXC": ("sbuf", [128, 16], "float32"), "SYC": ("sbuf", [128, 1], "float32"),
+    "MK": ("sbuf", [128, 128], "float32"), "LOW": ("sbuf", [128, 8], "int32"), "LW": ("sbuf", [128, 8], "uint16"),
     "SCI": ("sbuf", [128, 16], "int32"), "SCH": ("sbuf", [128, 16], "int32"), "SCL": ("sbuf", [128, 16], "int32"),
     "SCP": ("sbuf", [128, 16], "int32"), "LN": ("sbuf", [128, 16], "uint16"),
     "GM": ("sbuf", [128, 256], "float16"), "CL": ("sbuf", [128, 16], "uint16"), "CG": ("sbuf", [128, 256], "bfloat16"),
-    "CS": ("sbuf", [128, 32], "bfloat16"),
-    "I0A": ("sbuf", [128, 256], "float32"), "I0B": ("sbuf", [128, 256], "float32"), "I0F": ("sbuf", [128, 256], "float32"),
-    "JUNK": ("sbuf", [128, 32], "float32"), "EN": ("sbuf", [128, 2], "float32"), "RE": ("sbuf", [128, 16], "float32"),
-    "MN": ("sbuf", [128, 1], "float32"), "U": ("sbuf", [128, 16], "float32"), "SC": ("sbuf", [128, 16], "float32"),
-    "WT": ("sbuf", [128, 1], "float32"), "WK": ("sbuf", [128, 128], "float16"),
+    "CS": ("sbuf", [128, 32], "bfloat16"), "I0": ("sbuf", [128, 256], "float32"),
+    "SQ": ("sbuf", [128, 32], "float32"), "PM": ("sbuf", [128, 16], "float32"), "JUNK": ("sbuf", [128, 16], "float32"),
+    "AC": ("sbuf", [128, 1], "float32"), "WT": ("sbuf", [128, 1], "float32"), "WK": ("sbuf", [128, 128], "float16"),
     "IDX": ("sbuf", [128, 256], "uint16"), "F": ("sbuf", [128, 4096], "bfloat16"), "FS": ("sbuf", [128, 384], "bfloat16"),
     "YS": ("sbuf", [128, 128], "float32"),
     "PA": ("psum", [128, 512], "float32"), "PB": ("psum", [128, 512], "float32"), "PC": ("psum", [128, 512], "float32"),
-    "PY": ("psum", [128, 512], "float32"),
+    "PD": ("psum", [128, 512], "float32"), "PY": ("psum", [128, 512], "float32"),
 }
 for _q in range(N):
-    SCRATCH["Q%d" % _q] = ("psum", [128, 512], "float32")
     SCRATCH["CR%d" % _q] = ("sbuf", [128, 32], "bfloat16")
     SCRATCH["FR%d" % _q] = ("sbuf", [128, 128], "bfloat16")
+for _q in range(N - 1):
+    SCRATCH["Q%d" % _q] = ("psum", [128, 512], "float32")
 SEMAPHORES = ["v", "s", "p", "c", "dpos", "dta", "dtb", "dtr", "dw", "dy", "lc", "lf"]
 SEMAPHORES += ["ca%d" % _q for _q in range(N)] + ["fa%d" % _q for _q in range(N)]
 
@@ -83,6 +77,10 @@ def rank_program(g, core, T, topo):
     def cp(deps, out, in_): return V(deps, lambda e: e.tensor_copy(out, in_))
     def act(deps, out, in_, func, **kw): return op("s", deps, lambda e: e.activation(out, in_, func, **kw))
     def mm(deps, out, lhsT, rhs, start, stop): return op("p", deps, lambda e: e.matmul(out, lhsT, rhs, start, stop))
+    def iota(out, pattern, base, cm):
+        return op("c", [], lambda e: e.iota(out, pattern, base, cm, allow_small_or_imprecise_dtypes=True))
+    def pick(deps, out, in_, pattern, base):
+        return op("c", deps, lambda e: e.affine_select(out, in_, pattern, A.is_equal, 0.0, base, -1))
 
     others = sorted([q for q in range(N) if q != rank],
                     key=lambda q: (topo.same_plane(chip, topo.chip(cores[q])), q ^ rank))
@@ -94,90 +92,86 @@ def rank_program(g, core, T, topo):
     g.sync.dma_start(T.TR[:], T.tr[:]).then_inc(T.sem.dtr, 16)
     pos_in, ta_in, tb_in, tr_in = ("dpos", 16), ("dta", 16), ("dtb", 16), ("dtr", 16)
 
-    def iota(out, pattern, cm, flag):
-        if flag:
-            return op("c", [], lambda e: e.iota(out, pattern, 0, cm, allow_small_or_imprecise_dtypes=True))
-        return op("c", [], lambda e: e.iota(out, pattern, 0, cm))
-    k_p = iota(T.pI[:], [[0, 1]], 1, False)
-    k_c16 = iota(T.C16[:, 0:128], [[1, 8], [0, 16]], 0, True)
-    k_cf = iota(T.CF[:, 0:144], [[1, 144]], 0, True)
-    k_j16 = iota(T.J16[:], [[0, 8], [1, 16]], 0, True)
     a_one = V([], lambda e: e.memset(T.ONE[:], 1.0))
-    a_pf = cp([k_p], T.pF[:], T.pI[:])
+    k_p = op("c", [], lambda e: e.iota(T.pI[:], [[0, 1]], 0, 1))
+    a_bc = pick([a_one], T.BCT[0:8, :], T.ONE[0:8, 0:128], [[1, 8], [0, 16]], 0)
+    a_j16 = iota(T.J16[0:1, :], [[0, 8], [1, 16]], 0, 0)
+    a_ct = [iota(T.CT[:, 64 * t:64 * t + 64], [[1, 64]], 64 * q, 0) for t, q in enumerate(order)][-1]
+    a_idb = pick([], T.IDB[:], T.ONE[:, 0:128], [[1, 128]], 0)
+    a_idf = pick([], T.IDF[:], T.ONE[:, 0:128], [[1, 128]], 0)
+    a_c16 = iota(T.C16[0:16, :], [[0, 64]], 16, 0)
+    a_k16 = iota(T.k16[0:16, :], [[0, 1]], 0, 16)
+    a_rep = None
+    for t, q in enumerate(order):
+        a_rep = pick([a_c16], T.REP[0:16, 64 * t:64 * t + 64], T.C16[0:16, :], [[1, 4], [0, 16]], 4 * q)
     a_ri = ts([k_p], T.rI[:], T.pI[:], 15, None, A.bitwise_and)
-    a_ei = ts([k_p], T.eI[:], T.pI[:], 7, None, A.bitwise_and)
-    a_di = ts([k_p], T.dI[:], T.pI[:], 3, None, A.logical_shift_right)
+    a_cf = V([a_one], lambda e: e.tensor_tensor_scan(T.CF[:], T.ONE[:], T.ONE[:], -1.0, A.mult, A.add))
     a_rf = cp([a_ri], T.rF[:], T.rI[:])
-    a_bc = ts([k_c16, a_pf], T.BCT[0:8, :], T.C16[0:8, 0:128], T.pF[0:8, :], None, A.is_equal)
-    a_b16 = tt([a_pf, a_rf], T.b16[:], T.pF[:], T.rF[:], A.subtract)
-    a_ef = cp([a_ei], T.eF[:], T.eI[:])
-    a_df = cp([a_di], T.dF[:], T.dI[:])
-    a_c16 = act([k_c16], T.C16[0:16, 128:256], T.C16[0:16, 0:128], AF.Identity, bias=8.0)
-    a_k16 = act([a_pf], T.k16[:], T.pF[:], AF.Identity, scale=16.0)
-    a_r8 = act([a_rf], T.r8[:], T.rF[:], AF.Identity, scale=8.0)
-    a_cf = act([k_cf], T.CF[:, 144:256], T.CF[:, 32:144], AF.Identity, bias=112.0)
-    ts([], T.REP[0:16, 0:128], T.C16[0:16, 0:128], T.pF[0:16, :], 16.0, A.is_equal, A.mult)
-    a_rep = ts([a_c16], T.REP[0:16, 128:256], T.C16[0:16, 128:256], T.pF[0:16, :], 16.0, A.is_equal, A.mult)
-    a_lm = ts([k_cf, a_b16], T.LM[:], T.CF[:, 0:144], T.b16[:], 15.0, A.subtract, A.is_equal)
+    a_r32 = act([a_rf], T.r32[:], T.rF[:], AF.Identity, scale=32.0)
+    a_r8 = act([], T.r8[:], T.rF[:], AF.Identity, scale=8.0)
+    a_b16 = ts([a_rf], T.b16[:], T.pI[:], T.rF[:], None, A.subtract)
+    a_sel = ts([a_cf], T.SELP[:], T.CF[:, 0:48], T.rF[:], 16.0, A.subtract, A.is_equal)
+    a_pl = ts([a_r32], T.PL[:], T.CF[:, 0:32], T.r32[:], None, A.add)
+    a_lm = ts([a_b16], T.LM[:], T.CF[:, 0:144], T.b16[:], 15.0, A.subtract, A.is_equal)
+    SEL = T.SELP[:, 16:32]
     b_pos = ts([pos_in], T.POSB[0:8, :], T.POSI[0:8, :], -1.0, None, A.mult)
     b_nxy = mm([b_pos, a_bc], T.PA[:, 0:2], T.BCT[0:8, :], T.POSB[0:8, :], True, True)
+    s_xl = act([b_pos, a_one], T.XL[0:8, :], T.ONE[0:8, 0:16], AF.Identity, bias=T.POSB[0:8, 0:1], scale=0.0)
     s_xy8 = act([b_nxy], T.XY8[:], T.PA[:, 0:2], AF.Identity, bias=8.0)
     cx, cy = T.XY8[:, 0:1], T.XY8[:, 1:2]
-    s_sxc = act([s_xy8, k_cf], T.SXC[:], T.CF[:, 0:16], AF.Square, bias=cx, scale=16.0)
+    s_sxc = act([s_xy8, a_cf], T.SXC[:], T.CF[:, 0:16], AF.Square, bias=cx, scale=16.0)
     s_syc = act([a_rf], T.SYC[:], T.rF[:], AF.Square, bias=cy, scale=16.0)
-    s_sqx = act([k_c16], T.SQX[:], T.C16[:, 0:128], AF.Square, bias=cx, scale=16.0)
-    s_sqy = act([k_j16], T.PB[:, 0:128], T.J16[:], AF.Square, bias=cy, scale=16.0)
+    mm([s_xl], T.PY[0:16, 0:128], T.XL[0:8, :], T.BCT[0:8, :], True, False)
+    b_xp = mm([a_j16], T.PY[0:16, 0:128], T.ONE[0:1, 0:16], T.J16[0:1, :], False, True)
     t_a = ts([ta_in], T.X[:, :, 0:16], T.TIA[:], -2048.0, None, A.add)
-    a_m8 = ts([a_ef, k_cf], T.M8[:], T.CF[:, 0:8], T.eF[:], 7.0, A.add, A.is_equal)
     t_b = ts([tb_in], T.X[:, :, 16:32], T.TIB[:], -2048.0, None, A.add)
-    s_xyq = act([s_xy8], T.XYQ[:], T.XY8[:], AF.Identity, bias=-2.0, scale=0.25)
-    s_xq = act([s_xyq, a_rf], T.XQ[:], T.rF[:], AF.Square, bias=T.XYQ[:, 0:1], scale=0.25)
-    s_sqf = act([a_cf], T.SQF[:], T.CF[:], AF.Square, bias=T.XYQ[:, 1:2], scale=0.25)
-    s_xm = act([s_xq], T.XM[:], T.XQ[:], AF.Identity, bias=-0.46875)
-    s_xb = act([], T.XB[:], T.XYQ[:, 0:1], AF.Identity, scale=0.5)
-    s_ia = act([s_xm, s_sqf], T.I0A[:], T.SQF[:], AF.Identity, bias=T.XM[:])
-    b_xr = act([s_xb], T.XR[:], T.rF[:], AF.Identity, bias=T.XB[:], scale=0.125)
-    s_ib = act([s_ia], T.I0B[:], T.I0A[:], AF.Identity, bias=MAGIC)
-    s_i0 = act([s_ib], T.I0F[:], T.I0B[:], AF.Identity, bias=-MAGIC)
+    a_s8 = ts([], T.S8[:], T.CF[:, 0:8], 16.0, T.b16[:], A.mult, A.is_equal)
+    V([t_a, t_b], lambda e: e.transpose(T.XT[:, 0:TX], T.X[:, 0:TX // 32, :]))
     b_sc = ts([s_sxc, s_syc], T.SCI[:], T.SXC[:], T.SYC[:], None, A.add)
-    a_nk = ts([a_df], T.NK[:], T.CF[:, 0:16], T.dF[:], -1.0, A.is_equal, A.mult)
-    a_sb = ts([a_r8], T.SB[:], T.CF[:, 0:136], T.r8[:], 7.0, A.subtract, A.is_equal)
-    b_sr = tt([s_sqx, s_sqy], T.SR[:], T.PB[:, 0:128], T.SQX[:], A.add)
-    t_x = V([t_a, t_b], lambda e: e.transpose(T.XT[:], T.X[:]))
-    b_sh = ts([b_sc], T.SCH[:], T.SCI[:], 3, 480, A.logical_shift_right, A.bitwise_and)
-    b_sl = ts([b_sc], T.SCL[:], T.SCI[:], 12, None, A.logical_shift_right)
-    b_low = ts([b_sr], T.LOW[:], T.SR[:], 4, 15, A.logical_shift_right, A.bitwise_and)
+    t_x = V([], lambda e: e.transpose(T.XT[:, TX:512], T.X[:, TX // 32:16, :]))
+    b_low = ts([b_sc], T.LOW[:], T.SCI[:, 0:8], 4, 15, A.logical_shift_right, A.bitwise_and)
+    b_sh = ts([], T.SCH[:], T.SCI[:], 3, 480, A.logical_shift_right, A.bitwise_and)
+    b_sl = ts([], T.SCL[:], T.SCI[:], 12, None, A.logical_shift_right)
+    b_lw = cp([b_low], T.LW[:], T.LOW[:])
     b_sp = tt([b_sh, b_sl], T.SCP[:], T.SCH[:], T.SCL[:], A.add)
-    a_idb = ts([k_cf, a_pf], T.IDB[:], T.CF[:, 0:128], T.pF[:], None, A.is_equal)
-    b_mk = ts([b_low, a_rf], T.MK[:], T.LOW[:], T.rF[:], None, A.is_equal)
+    a_sb = ts([a_r8], T.SB[:], T.CF[:, 0:136], T.r8[:], 7.0, A.subtract, A.is_equal)
     b_ln = cp([b_sp], T.LN[:], T.SCP[:])
-    a_sel = ts([k_cf, a_rf], T.SEL[:], T.CF[:, 0:16], T.rF[:], None, A.is_equal)
-    a_idf = act([a_idb], T.IDF[:], T.IDB[:], AF.Identity)
-    b_dx = act([b_xr], T.DX[:], T.IDB[:], AF.Identity, scale=T.XR[:])
+    s_xyq = act([s_xy8], T.XYQ[:], T.XY8[:], AF.Identity, bias=-2.0, scale=0.25)
+    s_xp = act([b_xp], T.XP[0:16, :], T.PY[0:16, 0:128], AF.Identity, scale=0.125)
+    s_xq = act([s_xyq], T.XQ[:], T.rF[:], AF.Square, bias=T.XYQ[:, 0:1], scale=0.25)
+    s_i0 = act([a_ct], T.I0[:], T.CT[:], AF.Square, bias=T.XYQ[:, 1:2], scale=0.25)
+    s_xm = act([s_xq], T.XM[:], T.XQ[:], AF.Identity, bias=-0.46875)
+
+    def natural(a, e):
+        return act([t_x, a_pl], T.W[:, a:e], T.XT[:, 0:512].indirect(T.PL[:, a // 16:e // 16]), AF.Identity, bias=2048.0)
+    s_w = [natural(0, WA)] if WF else []
+    b_mk = act([b_lw, a_sel], T.MK[:], SEL.indirect(T.LW[:, 0:8]), AF.Copy)
+    s_w = s_w or [natural(0, WA)]
+    s_w.append(natural(WA, 512))
     c_gm = [tt([t_x, b_ln, b_mk], T.GM[:, h:h + 128], T.XT[:, 0:512].indirect(T.LN[:, h // 16:h // 16 + 8]), T.MK[:], A.mult)
             for h in (0, 128)]
     c_re = None
     for r in range(16):
         c_re = mm([c_gm[r // 8], a_lm], T.PC[:, 0:16], T.LM[:, 15 - r:143 - r], T.GM[:, 16 * r:16 * r + 16], r == 0, r == 15)
-    def times(b): return ts([t_x], T.OL[:, b:512:16], T.XT[:, 32 * b:32 * b + 32], 2048.0, None, A.add)
-    t_ol = None
-    for b in range(OLB):
-        times(b)
-    c_cl = ts([c_re], T.CL[:], T.PC[:, 0:16], 2048.0, None, A.add)
-    for b in range(OLB, 16):
-        t_ol = times(b)
+    t_ol = [cp([s_w[0]], T.OL[:, 0:WA], T.W[:, 0:WA])]
     col, last = [0], {}
 
     def piece(q, n):
         a, e = col[0], col[0] + n
         col[0] = e
         out, in_ = T.T2[:, 16 * a:16 * e], T.TR[:, 0:4096].indirect(T.OL[:, a:e])
-        last[q] = cp([t_ol, tr_in], out, in_) if q == "v" else act([t_ol, tr_in], out, in_, AF.Copy)
+        deps = [t_ol[1 if e > WA else 0], tr_in]
+        last[q] = cp(deps, out, in_) if q == "v" else act(deps, out, in_, AF.Copy)
+    piece("v", T2A)
+    piece("s", T2B)
+    c_cl = ts([c_re], T.CL[:], T.PC[:, 0:16], 2048.0, None, A.add)
     c_gv = cp([tr_in, c_cl], T.CG[:, 0:128], T.TR[:, 0:4096].indirect(T.CL[:, 0:8]))
     c_gs = act([tr_in, c_cl], T.CG[:, 128:256], T.TR[:, 0:4096].indirect(T.CL[:, 8:16]), AF.Copy)
-    mm([c_gv, c_gs, a_sel], T.PC[:, 32:48], T.CG[:, 0:256:2], T.SEL[:], True, True)
-    c_ps = mm([], T.PC[:, 48:64], T.CG[:, 1:256:2], T.SEL[:], True, True)
-    piece("v", T2V0)
+    c_ps = None
+    for a in range(8):
+        h, u = a // 2, a % 2
+        c_ps = mm([c_gv, c_gs], T.PC[32 * h:32 * h + 32, 32:64], T.SELP[:, 16 - 16 * u:48 - 16 * u], T.CG[:, a:256:8], u == 0, u == 1)
+    t_ol.append(cp([s_w[1]], T.OL[:, WA:512], T.W[:, WA:512]))
     c_cs = cp([c_ps], T.CS[:], T.PC[:, 32:64])
     mask = 0xFFFF
     for q in others:
@@ -191,90 +185,68 @@ def rank_program(g, core, T, topo):
     g.remote_dma_fused([RemoteDMATransfer(dst_ids=[dst(q) for q in others], dma_engine_mask=mask, remote_sem=T.sem["ca%d" % rank],
                                           srcs=[T.CS[:]], dsts=[T["CR%d" % rank][:] for q in others], alu_op=0)],
                        local_sem=T.sem.lc)
-    for n in T2V:
-        piece("v", n)
-    for n in T2S:
-        piece("s", n)
-    b_xp = mm([b_dx, a_one], T.PA[0:16, 128:256], T.ONE[:], T.DX[:], True, True)
-    e_a = mm([c_cs, a_idb], T.PB[:, 256:288], T.IDB[:], T.CS[:], True, False)
-    for t, q in enumerate(order):
-        mm([s_i0, a_idf], T["Q%d" % t][:, 0:64], T.IDF[:], T.I0F[:, 64 * q:64 * q + 64], True, False)
+    piece("s", T2S)
+    piece("v", T2V)
+    e_a = mm([c_cs, a_idb], T.PB[:, 0:32], T.IDB[:], T.CS[:], True, False)
+    PI, CUT = [T.PA[:, 256:320], T.PD[:, 0:128], T.PC[:, 128:192]], (0, 64, 192, 256)
+    for n in range(3):
+        mm([s_i0, a_idf, s_xp], PI[n], T.IDF[:], T.I0[:, CUT[n]:CUT[n + 1]], True, False)
     for n, q in enumerate(others):
-        e_a = mm([("ca%d" % q, n_e)], T.PB[:, 256:288], T.IDB[:], T["CR%d" % q][:], False, n == N - 2)
-    e_0 = act([e_a], T.JUNK[:, 0:16], T.PB[:, 256:272], AF.Square, accum_out=T.EN[:, 0:1])
-    e_1 = act([], T.JUNK[:, 16:32], T.PB[:, 272:288], AF.Square, accum_out=T.EN[:, 1:2])
-    piece("s", TOT - col[0] - T2V1 - 3 * T2M - T2V2)
-    ts([e_0, a_m8], T.RE[:, 1:16:2], T.M8[:], T.EN[:, 0:1], None, A.mult)
-    e_r = ts([e_1], T.RE[:, 0:16:2], T.M8[:], T.EN[:, 1:2], None, A.mult)
-    e_e = mm([e_r, a_nk], T.PB[0:16, 320:336], T.NK[:], T.RE[:], True, True)
+        e_a = mm([("ca%d" % q, n_e)], T.PB[:, 0:32], T.IDB[:], T["CR%d" % q][:], False, n == N - 2)
+    e_q = act([e_a], T.SQ[:], T.PB[:, 0:32], AF.Square)
+    piece("s", T2S1)
+    e_e = None
+    for u in range(2):
+        e_e = mm([e_q, a_s8], T.PB[0:16, 64 + 8 * u:72 + 8 * u], T.SQ[:, u:32:2], T.S8[:], True, True)
+    w_m = V([e_e], lambda e: e.tensor_tensor_scan(T.PM[0:16, :], T.PB[0:16, 64:80], T.ONE[0:16, 0:16], 0.0, A.max, A.mult))
     piece("v", T2V1)
-    w_m = V([e_e], lambda e: e.tensor_reduce(T.MN[0:16, :], T.PB[0:16, 320:336], AxisListType.X, A.min))
-    piece("v", T2M)
-    w_u = ts([w_m], T.U[0:16, :], T.PB[0:16, 320:336], T.MN[0:16, :], 1.0, A.subtract, A.min)
-    piece("v", T2M)
-    w_s = V([w_u], lambda e: e.tensor_tensor_scan(T.SC[0:16, :], T.U[0:16, :], T.U[0:16, :], 0.0, A.mult, A.add))
-    piece("v", T2M)
-    acol = T.SC[0:16, 15:16]
-    w_k = ts([w_s, b_xp], T.WK[0:16, :], T.PA[0:16, 128:256], acol, acol, A.add, A.mult)
-    piece("v", T2V2)
-    i_q = []
-    for t, q in enumerate(order):
-        i_q.append(mm([w_k, a_rep], T["Q%d" % t][:, 0:64], T.WK[0:16, :], T.REP[0:16, 64 * q:64 * q + 64], False, True))
-    idx, got, fp, fs = [], [{} for _ in range(N)], [None] * N, [None] * N
+    acol = T.AC[0:16, :]
+    w_s = act([w_m], T.JUNK[0:16, :], T.PM[0:16, :], AF.Sign, bias=T.PM[0:16, 15:16], scale=-1.0, accum_out=acol)
+    piece("s", TOT - col[0] - T2V2 - 1)
+    w_k = ts([w_s, s_xp], T.WK[0:16, :], T.XP[0:16, :], acol, acol, A.add, A.mult)
+    piece("v", T2V2 + 1)
+    i_q = [mm([w_k, a_rep], PI[n], T.WK[0:16, :], T.REP[0:16, CUT[n]:CUT[n + 1]], False, True) for n in range(3)]
 
-    def index(t):
-        q = order[t]
-        idx.append(cp([i_q[t]], T.IDX[:, 64 * q:64 * q + 64], T["Q%d" % t][:, 0:64]))
+    def index(n): return ts([i_q[n], s_xm], T.IDX[:, CUT[n]:CUT[n + 1]], PI[n], T.XM[:], None, A.add)
+    idx = [index(0)]
+    idx += [index(1)] * 2
+    got, nxt = [{} for _ in range(N)], [0] * N
 
-    def gather(t, kind, part):
-        q, parts = order[t], PARTS[t] if kind == "v" else PARTS_S[t]
-        b = sum(parts[:part]) + (0 if kind == "v" else sum(PARTS[t]))
-        lo, hi = 64 * q + 8 * b, 64 * q + 8 * (b + parts[part])
+    def gather(kind, t, n):
+        b = nxt[t]
+        nxt[t] = b + n
+        lo, hi = 64 * t + 8 * b, 64 * t + 8 * (b + n)
         deps, out, in_ = [idx[t], last["v"], last["s"]], T.F[:, 16 * lo:16 * hi], T.T2[:, 0:16 * TOT].indirect(T.IDX[:, lo:hi])
         c = cp(deps, out, in_) if kind == "v" else act(deps, out, in_, AF.Copy)
-        for i in range(b, b + parts[part]):
+        for i in range(b, b + n):
             got[t][i] = c
 
-    def gathers(t, kind):
-        for part in range(len(PARTS[t] if kind == "v" else PARTS_S[t])):
-            gather(t, kind, part)
-
-    def blocks(t):
-        base = {k: min(c[1] for c in got[t].values() if c[0] == k) for k in "vs"}
-        return sorted(range(8), key=lambda b: (got[t][b][1] != base[got[t][b][0]], got[t][b][0], b))
-
-    def sums(t):
-        q = order[t]
-        for b in blocks(t):
-            fp[t] = mm([got[t][b], a_sel], T["Q%d" % t][:, 128 + b:256:8],
-                       T.F[:, 1024 * q + 128 * b:1024 * q + 128 * b + 128], T.SEL[:], True, True)
-
-    def out(t):
-        q = order[t]
-        fs[t] = cp([fp[t]], T.FS[:, 128 * t:128 * t + 128], T["Q%d" % t][:, 128:256])
-        wait("c", fs[t])
+    def send(kind, t):
+        q, fp = order[t], None
+        for b in range(8):
+            fp = mm([got[t][b]], T["Q%d" % t][:, b:128:8], T.F[:, 1024 * t + 128 * b:1024 * t + 128 * b + 128], SEL, True, True)
+        out, in_ = T.FS[:, 128 * t:128 * t + 128], T["Q%d" % t][:, 0:128]
+        wait("c", cp([fp], out, in_) if kind == "v" else act([fp], out, in_, AF.Copy))
         rid, pid, _ = topo.addr(cores[q])
-        g.remote_dma(T["FR%d" % rank][:], T.FS[:, 128 * t:128 * t + 128], T.sem["fa%d" % rank], T.sem.lf, pid, rid,
-                     topo.mask(core, cores[q]))
-    index(0); index(1); index(2); index(3)
-    gathers(0, "v"); gathers(0, "s")
-    sums(0)
-    for t in (1, 2, 3):
-        gather(t, "v", 0)
-        out(t - 1)
-        gather(t, "v", 1)
-        gathers(t, "s")
-        if t < 3:
-            sums(t)
-    w_t = ts([a_k16], T.WT[0:16, :], acol, T.k16[0:16, :], None, A.add)
+        g.remote_dma(T["FR%d" % rank][:], out, T.sem["fa%d" % rank], T.sem.lf, pid, rid, topo.mask(core, cores[q]))
+    for kind, t, n in FINE:
+        if t == len(idx):
+            idx.append(index(2))
+        if n:
+            gather(kind, t, n)
+        else:
+            send(kind, t)
+    w_t = act([a_k16], T.WT[0:16, :], acol, AF.Identity, bias=T.k16[0:16, :])
     wait("y", w_t)
     g.sync.dma_start(T.w[:], T.WT[0:16, :]).then_inc(T.sem.dw, 16)
-    for n, b in enumerate(blocks(3)):
-        mm([got[3][b], a_sb], T.PY[:, 0:128], T.SB[:, 7 - b:135 - b],
-           T.F[:, 1024 * rank + 128 * b:1024 * rank + 128 * b + 128], n == 0, False)
     y_p = None
-    for n, q in enumerate(others):
-        y_p = mm([("fa%d" % q, bin(topo.mask(cores[q], core)).count("1"))], T.PY[:, 0:128], T["FR%d" % q][:], T.IDB[:], False, n == N - 2)
+    for b in range(9):
+        for n, q in enumerate(others):
+            if ARR[n] == b:
+                y_p = mm([("fa%d" % q, bin(topo.mask(cores[q], core)).count("1"))], T.PY[:, 0:128], T["FR%d" % q][:], T.IDB[:],
+                         False, n == N - 2)
+        if b < 8:
+            mm([got[3][b], a_sb], T.PY[:, 0:128], T.SB[:, 7 - b:135 - b], T.F[:, 3072 + 128 * b:3072 + 128 * b + 128], b == 0, False)
     y_s = cp([y_p], T.YS[:], T.PY[:, 0:128])
     wait("y", y_s)
     g.sync.dma_start(T.y[:], T.YS[:]).then_inc(T.sem.dy, 16)

from concourse.bass import DstId, RemoteDMATransfer
from concourse.mybir import AluOpType as A, ActivationFunctionType as AF

N = 4
TOT = 509
T2A, T2B = 16, 24
T2V, T2V1, T2V2 = 196, 10, 12
T2S, T2S1 = 196, 22
WA, WF, TX = 256, 0, 256
FINE = [("s", 0, 4), ("v", 0, 4), ("s", 1, 4), ("v", 1, 4), ("v", 0, 0), ("s", 2, 1), ("v", 2, 3), ("s", 2, 3),
        ("v", 2, 1), ("s", 1, 0), ("s", 3, 3), ("v", 2, 0), ("s", 3, 2), ("v", 3, 3)]
ARR = (3, 8, 8)
SCRATCH = {
    "TR": ("sbuf", [128, 4096], "bfloat16"), "T2": ("sbuf", [128, 8192], "bfloat16"),
    "TIA": ("sbuf", [128, 16, 16], "int32"), "TIB": ("sbuf", [128, 16, 16], "int32"), "X": ("sbuf", [128, 16, 32], "float32"),
    "XT": ("sbuf", [128, 512], "float32"), "W": ("sbuf", [128, 512], "float32"), "OL": ("sbuf", [128, 512], "uint16"),
    "POSI": ("sbuf", [128, 2], "int32"), "POSB": ("sbuf", [128, 2], "bfloat16"), "PL": ("sbuf", [128, 32], "uint16"),
    "pI": ("sbuf", [128, 1], "int32"), "rI": ("sbuf", [128, 1], "int32"), "rF": ("sbuf", [128, 1], "float32"),
    "b16": ("sbuf", [128, 1], "float32"), "k16": ("sbuf", [128, 1], "float32"), "r8": ("sbuf", [128, 1], "float32"),
    "r32": ("sbuf", [128, 1], "float32"), "CT": ("sbuf", [128, 256], "bfloat16"), "J16": ("sbuf", [128, 128], "bfloat16"),
    "CF": ("sbuf", [128, 144], "bfloat16"), "ONE": ("sbuf", [128, 144], "bfloat16"), "C16": ("sbuf", [128, 64], "bfloat16"),
    "IDF": ("sbuf", [128, 128], "float32"), "IDB": ("sbuf", [128, 128], "bfloat16"), "SELP": ("sbuf", [128, 48], "bfloat16"),
    "BCT": ("sbuf", [128, 128], "bfloat16"), "S8": ("sbuf", [128, 8], "float32"),
    "REP": ("sbuf", [128, 256], "bfloat16"), "LM": ("sbuf", [128, 144], "float16"), "SB": ("sbuf", [128, 136], "bfloat16"),
    "XY8": ("sbuf", [128, 2], "float32"), "XYQ": ("sbuf", [128, 2], "float32"), "XL": ("sbuf", [128, 16], "bfloat16"),
    "XQ": ("sbuf", [128, 1], "float32"), "XM": ("sbuf", [128, 1], "float32"), "XP": ("sbuf", [128, 128], "bfloat16"),
    "SXC": ("sbuf", [128, 16], "float32"), "SYC": ("sbuf", [128, 1], "float32"),
    "MK": ("sbuf", [128, 128], "float32"), "LOW": ("sbuf", [128, 8], "int32"), "LW": ("sbuf", [128, 8], "uint16"),
    "SCI": ("sbuf", [128, 16], "int32"), "SCH": ("sbuf", [128, 16], "int32"), "SCL": ("sbuf", [128, 16], "int32"),
    "SCP": ("sbuf", [128, 16], "int32"), "LN": ("sbuf", [128, 16], "uint16"),
    "GM": ("sbuf", [128, 256], "float16"), "CL": ("sbuf", [128, 16], "uint16"), "CG": ("sbuf", [128, 256], "bfloat16"),
    "CS": ("sbuf", [128, 32], "bfloat16"), "I0": ("sbuf", [128, 256], "float32"),
    "SQ": ("sbuf", [128, 32], "float32"), "PM": ("sbuf", [128, 16], "float32"), "JUNK": ("sbuf", [128, 16], "float32"),
    "AC": ("sbuf", [128, 1], "float32"), "WT": ("sbuf", [128, 1], "float32"), "WK": ("sbuf", [128, 128], "float16"),
    "IDX": ("sbuf", [128, 256], "uint16"), "F": ("sbuf", [128, 4096], "bfloat16"), "FS": ("sbuf", [128, 384], "bfloat16"),
    "YS": ("sbuf", [128, 128], "float32"),
    "PA": ("psum", [128, 512], "float32"), "PB": ("psum", [128, 512], "float32"), "PC": ("psum", [128, 512], "float32"),
    "PD": ("psum", [128, 512], "float32"), "PY": ("psum", [128, 512], "float32"),
}
for _q in range(N):
    SCRATCH["CR%d" % _q] = ("sbuf", [128, 32], "bfloat16")
    SCRATCH["FR%d" % _q] = ("sbuf", [128, 128], "bfloat16")
for _q in range(N - 1):
    SCRATCH["Q%d" % _q] = ("psum", [128, 512], "float32")
SEMAPHORES = ["v", "s", "p", "c", "dpos", "dta", "dtb", "dtr", "dw", "dy", "lc", "lf"]
SEMAPHORES += ["ca%d" % _q for _q in range(N)] + ["fa%d" % _q for _q in range(N)]


def rank_program(g, core, T, topo):
    rank = T.rank_of(core)
    if rank is None:
        return
    cores = T.cores
    chip = topo.chip(core)
    queue = {"v": g.vector, "s": g.scalar, "p": g.tensor, "c": g, "y": g.sync}
    count = {"v": 0, "s": 0, "p": 0, "c": 0}
    seen = {}

    def wait(q, *deps):
        for name, val in deps:
            if seen.get((q, name), 0) < val:
                seen[(q, name)] = val
                queue[q].wait_ge(T.sem[name], val)

    def op(q, deps, make):
        wait(q, *deps)
        make(queue[q]).then_inc(T.sem[q], 1)
        count[q] += 1
        return (q, count[q])

    def V(deps, make): return op("v", deps, make)
    def ts(deps, out, in0, s1, s2, o0, o1=None):
        if o1 is None:
            return V(deps, lambda e: e.tensor_scalar(out, in0, s1, None, o0))
        return V(deps, lambda e: e.tensor_scalar(out, in0, s1, s2, o0, o1))
    def tt(deps, out, a, b, o): return V(deps, lambda e: e.tensor_tensor(out, a, b, o))
    def cp(deps, out, in_): return V(deps, lambda e: e.tensor_copy(out, in_))
    def act(deps, out, in_, func, **kw): return op("s", deps, lambda e: e.activation(out, in_, func, **kw))
    def mm(deps, out, lhsT, rhs, start, stop): return op("p", deps, lambda e: e.matmul(out, lhsT, rhs, start, stop))
    def iota(out, pattern, base, cm):
        return op("c", [], lambda e: e.iota(out, pattern, base, cm, allow_small_or_imprecise_dtypes=True))
    def pick(deps, out, in_, pattern, base):
        return op("c", deps, lambda e: e.affine_select(out, in_, pattern, A.is_equal, 0.0, base, -1))

    others = sorted([q for q in range(N) if q != rank],
                    key=lambda q: (topo.same_plane(chip, topo.chip(cores[q])), q ^ rank))
    order = others + [rank]

    g.sync.dma_start(T.POSI[0:8, :], T.pos[:]).then_inc(T.sem.dpos, 16)
    g.scalar.dma_start(T.TIA[:], T.tau[0:8:2, :]).then_inc(T.sem.dta, 16)
    g.sync.dma_start(T.TIB[:], T.tau[1:8:2, :]).then_inc(T.sem.dtb, 16)
    g.sync.dma_start(T.TR[:], T.tr[:]).then_inc(T.sem.dtr, 16)
    pos_in, ta_in, tb_in, tr_in = ("dpos", 16), ("dta", 16), ("dtb", 16), ("dtr", 16)

    a_one = V([], lambda e: e.memset(T.ONE[:], 1.0))
    k_p = op("c", [], lambda e: e.iota(T.pI[:], [[0, 1]], 0, 1))
    a_bc = pick([a_one], T.BCT[0:8, :], T.ONE[0:8, 0:128], [[1, 8], [0, 16]], 0)
    a_j16 = iota(T.J16[0:1, :], [[0, 8], [1, 16]], 0, 0)
    a_ct = [iota(T.CT[:, 64 * t:64 * t + 64], [[1, 64]], 64 * q, 0) for t, q in enumerate(order)][-1]
    a_idb = pick([], T.IDB[:], T.ONE[:, 0:128], [[1, 128]], 0)
    a_idf = pick([], T.IDF[:], T.ONE[:, 0:128], [[1, 128]], 0)
    a_c16 = iota(T.C16[0:16, :], [[0, 64]], 16, 0)
    a_k16 = iota(T.k16[0:16, :], [[0, 1]], 0, 16)
    a_rep = None
    for t, q in enumerate(order):
        a_rep = pick([a_c16], T.REP[0:16, 64 * t:64 * t + 64], T.C16[0:16, :], [[1, 4], [0, 16]], 4 * q)
    a_ri = ts([k_p], T.rI[:], T.pI[:], 15, None, A.bitwise_and)
    a_cf = V([a_one], lambda e: e.tensor_tensor_scan(T.CF[:], T.ONE[:], T.ONE[:], -1.0, A.mult, A.add))
    a_rf = cp([a_ri], T.rF[:], T.rI[:])
    a_r32 = act([a_rf], T.r32[:], T.rF[:], AF.Identity, scale=32.0)
    a_r8 = act([], T.r8[:], T.rF[:], AF.Identity, scale=8.0)
    a_b16 = ts([a_rf], T.b16[:], T.pI[:], T.rF[:], None, A.subtract)
    a_sel = ts([a_cf], T.SELP[:], T.CF[:, 0:48], T.rF[:], 16.0, A.subtract, A.is_equal)
    a_pl = ts([a_r32], T.PL[:], T.CF[:, 0:32], T.r32[:], None, A.add)
    a_lm = ts([a_b16], T.LM[:], T.CF[:, 0:144], T.b16[:], 15.0, A.subtract, A.is_equal)
    SEL = T.SELP[:, 16:32]
    b_pos = ts([pos_in], T.POSB[0:8, :], T.POSI[0:8, :], -1.0, None, A.mult)
    b_nxy = mm([b_pos, a_bc], T.PA[:, 0:2], T.BCT[0:8, :], T.POSB[0:8, :], True, True)
    s_xl = act([b_pos, a_one], T.XL[0:8, :], T.ONE[0:8, 0:16], AF.Identity, bias=T.POSB[0:8, 0:1], scale=0.0)
    s_xy8 = act([b_nxy], T.XY8[:], T.PA[:, 0:2], AF.Identity, bias=8.0)
    cx, cy = T.XY8[:, 0:1], T.XY8[:, 1:2]
    s_sxc = act([s_xy8, a_cf], T.SXC[:], T.CF[:, 0:16], AF.Square, bias=cx, scale=16.0)
    s_syc = act([a_rf], T.SYC[:], T.rF[:], AF.Square, bias=cy, scale=16.0)
    mm([s_xl], T.PY[0:16, 0:128], T.XL[0:8, :], T.BCT[0:8, :], True, False)
    b_xp = mm([a_j16], T.PY[0:16, 0:128], T.ONE[0:1, 0:16], T.J16[0:1, :], False, True)
    t_a = ts([ta_in], T.X[:, :, 0:16], T.TIA[:], -2048.0, None, A.add)
    t_b = ts([tb_in], T.X[:, :, 16:32], T.TIB[:], -2048.0, None, A.add)
    a_s8 = ts([], T.S8[:], T.CF[:, 0:8], 16.0, T.b16[:], A.mult, A.is_equal)
    V([t_a, t_b], lambda e: e.transpose(T.XT[:, 0:TX], T.X[:, 0:TX // 32, :]))
    b_sc = ts([s_sxc, s_syc], T.SCI[:], T.SXC[:], T.SYC[:], None, A.add)
    t_x = V([], lambda e: e.transpose(T.XT[:, TX:512], T.X[:, TX // 32:16, :]))
    b_low = ts([b_sc], T.LOW[:], T.SCI[:, 0:8], 4, 15, A.logical_shift_right, A.bitwise_and)
    b_sh = ts([], T.SCH[:], T.SCI[:], 3, 480, A.logical_shift_right, A.bitwise_and)
    b_sl = ts([], T.SCL[:], T.SCI[:], 12, None, A.logical_shift_right)
    b_lw = cp([b_low], T.LW[:], T.LOW[:])
    b_sp = tt([b_sh, b_sl], T.SCP[:], T.SCH[:], T.SCL[:], A.add)
    a_sb = ts([a_r8], T.SB[:], T.CF[:, 0:136], T.r8[:], 7.0, A.subtract, A.is_equal)
    b_ln = cp([b_sp], T.LN[:], T.SCP[:])
    s_xyq = act([s_xy8], T.XYQ[:], T.XY8[:], AF.Identity, bias=-2.0, scale=0.25)
    s_xp = act([b_xp], T.XP[0:16, :], T.PY[0:16, 0:128], AF.Identity, scale=0.125)
    s_xq = act([s_xyq], T.XQ[:], T.rF[:], AF.Square, bias=T.XYQ[:, 0:1], scale=0.25)
    s_i0 = act([a_ct], T.I0[:], T.CT[:], AF.Square, bias=T.XYQ[:, 1:2], scale=0.25)
    s_xm = act([s_xq], T.XM[:], T.XQ[:], AF.Identity, bias=-0.46875)

    def natural(a, e):
        return act([t_x, a_pl], T.W[:, a:e], T.XT[:, 0:512].indirect(T.PL[:, a // 16:e // 16]), AF.Identity, bias=2048.0)
    s_w = [natural(0, WA)] if WF else []
    b_mk = act([b_lw, a_sel], T.MK[:], SEL.indirect(T.LW[:, 0:8]), AF.Copy)
    s_w = s_w or [natural(0, WA)]
    s_w.append(natural(WA, 512))
    c_gm = [tt([t_x, b_ln, b_mk], T.GM[:, h:h + 128], T.XT[:, 0:512].indirect(T.LN[:, h // 16:h // 16 + 8]), T.MK[:], A.mult)
            for h in (0, 128)]
    c_re = None
    for r in range(16):
        c_re = mm([c_gm[r // 8], a_lm], T.PC[:, 0:16], T.LM[:, 15 - r:143 - r], T.GM[:, 16 * r:16 * r + 16], r == 0, r == 15)
    t_ol = [cp([s_w[0]], T.OL[:, 0:WA], T.W[:, 0:WA])]
    col, last = [0], {}

    def piece(q, n):
        a, e = col[0], col[0] + n
        col[0] = e
        out, in_ = T.T2[:, 16 * a:16 * e], T.TR[:, 0:4096].indirect(T.OL[:, a:e])
        deps = [t_ol[1 if e > WA else 0], tr_in]
        last[q] = cp(deps, out, in_) if q == "v" else act(deps, out, in_, AF.Copy)
    piece("v", T2A)
    piece("s", T2B)
    c_cl = ts([c_re], T.CL[:], T.PC[:, 0:16], 2048.0, None, A.add)
    c_gv = cp([tr_in, c_cl], T.CG[:, 0:128], T.TR[:, 0:4096].indirect(T.CL[:, 0:8]))
    c_gs = act([tr_in, c_cl], T.CG[:, 128:256], T.TR[:, 0:4096].indirect(T.CL[:, 8:16]), AF.Copy)
    c_ps = None
    for a in range(8):
        h, u = a // 2, a % 2
        c_ps = mm([c_gv, c_gs], T.PC[32 * h:32 * h + 32, 32:64], T.SELP[:, 16 - 16 * u:48 - 16 * u], T.CG[:, a:256:8], u == 0, u == 1)
    t_ol.append(cp([s_w[1]], T.OL[:, WA:512], T.W[:, WA:512]))
    c_cs = cp([c_ps], T.CS[:], T.PC[:, 32:64])
    mask = 0xFFFF
    for q in others:
        mask &= topo.mask(core, cores[q])
    n_e = bin(mask).count("1")

    def dst(q):
        rid, pid, _ = topo.addr(cores[q])
        return DstId(rid=rid, pnc=pid)
    wait("c", c_cs)
    g.remote_dma_fused([RemoteDMATransfer(dst_ids=[dst(q) for q in others], dma_engine_mask=mask, remote_sem=T.sem["ca%d" % rank],
                                          srcs=[T.CS[:]], dsts=[T["CR%d" % rank][:] for q in others], alu_op=0)],
                       local_sem=T.sem.lc)
    piece("s", T2S)
    piece("v", T2V)
    e_a = mm([c_cs, a_idb], T.PB[:, 0:32], T.IDB[:], T.CS[:], True, False)
    PI, CUT = [T.PA[:, 256:320], T.PD[:, 0:128], T.PC[:, 128:192]], (0, 64, 192, 256)
    for n in range(3):
        mm([s_i0, a_idf, s_xp], PI[n], T.IDF[:], T.I0[:, CUT[n]:CUT[n + 1]], True, False)
    for n, q in enumerate(others):
        e_a = mm([("ca%d" % q, n_e)], T.PB[:, 0:32], T.IDB[:], T["CR%d" % q][:], False, n == N - 2)
    e_q = act([e_a], T.SQ[:], T.PB[:, 0:32], AF.Square)
    piece("s", T2S1)
    e_e = None
    for u in range(2):
        e_e = mm([e_q, a_s8], T.PB[0:16, 64 + 8 * u:72 + 8 * u], T.SQ[:, u:32:2], T.S8[:], True, True)
    w_m = V([e_e], lambda e: e.tensor_tensor_scan(T.PM[0:16, :], T.PB[0:16, 64:80], T.ONE[0:16, 0:16], 0.0, A.max, A.mult))
    piece("v", T2V1)
    acol = T.AC[0:16, :]
    w_s = act([w_m], T.JUNK[0:16, :], T.PM[0:16, :], AF.Sign, bias=T.PM[0:16, 15:16], scale=-1.0, accum_out=acol)
    piece("s", TOT - col[0] - T2V2 - 1)
    w_k = ts([w_s, s_xp], T.WK[0:16, :], T.XP[0:16, :], acol, acol, A.add, A.mult)
    piece("v", T2V2 + 1)
    i_q = [mm([w_k, a_rep], PI[n], T.WK[0:16, :], T.REP[0:16, CUT[n]:CUT[n + 1]], False, True) for n in range(3)]

    def index(n): return ts([i_q[n], s_xm], T.IDX[:, CUT[n]:CUT[n + 1]], PI[n], T.XM[:], None, A.add)
    idx = [index(0)]
    idx += [index(1)] * 2
    got, nxt = [{} for _ in range(N)], [0] * N

    def gather(kind, t, n):
        b = nxt[t]
        nxt[t] = b + n
        lo, hi = 64 * t + 8 * b, 64 * t + 8 * (b + n)
        deps, out, in_ = [idx[t], last["v"], last["s"]], T.F[:, 16 * lo:16 * hi], T.T2[:, 0:16 * TOT].indirect(T.IDX[:, lo:hi])
        c = cp(deps, out, in_) if kind == "v" else act(deps, out, in_, AF.Copy)
        for i in range(b, b + n):
            got[t][i] = c

    def send(kind, t):
        q, fp = order[t], None
        for b in range(8):
            fp = mm([got[t][b]], T["Q%d" % t][:, b:128:8], T.F[:, 1024 * t + 128 * b:1024 * t + 128 * b + 128], SEL, True, True)
        out, in_ = T.FS[:, 128 * t:128 * t + 128], T["Q%d" % t][:, 0:128]
        wait("c", cp([fp], out, in_) if kind == "v" else act([fp], out, in_, AF.Copy))
        rid, pid, _ = topo.addr(cores[q])
        g.remote_dma(T["FR%d" % rank][:], out, T.sem["fa%d" % rank], T.sem.lf, pid, rid, topo.mask(core, cores[q]))
    for kind, t, n in FINE:
        if t == len(idx):
            idx.append(index(2))
        if n:
            gather(kind, t, n)
        else:
            send(kind, t)
    w_t = act([a_k16], T.WT[0:16, :], acol, AF.Identity, bias=T.k16[0:16, :])
    wait("y", w_t)
    g.sync.dma_start(T.w[:], T.WT[0:16, :]).then_inc(T.sem.dw, 16)
    y_p = None
    for b in range(9):
        for n, q in enumerate(others):
            if ARR[n] == b:
                y_p = mm([("fa%d" % q, bin(topo.mask(cores[q], core)).count("1"))], T.PY[:, 0:128], T["FR%d" % q][:], T.IDB[:],
                         False, n == N - 2)
        if b < 8:
            mm([got[3][b], a_sb], T.PY[:, 0:128], T.SB[:, 7 - b:135 - b], T.F[:, 3072 + 128 * b:3072 + 128 * b + 128], b == 0, False)
    y_s = cp([y_p], T.YS[:], T.PY[:, 0:128])
    wait("y", y_s)
    g.sync.dma_start(T.y[:], T.YS[:]).then_inc(T.sem.dy, 16)
    wait("y", ("dw", 16), ("dy", 16))
    lf = sum(bin(topo.mask(core, cores[q])).count("1") for q in others)
    wait("c", ("lc", n_e), ("lf", lf))
    wait("c", ("v", count["v"]), ("s", count["s"]), ("p", count["p"]), ("c", count["c"]))
